import numpy as np
import ml_dtypes


def mxq(x, axis, fmt="e4m3"):
    dtype, down = {"e4m3": (ml_dtypes.float8_e4m3fn, 7), "e5m2": (ml_dtypes.float8_e5m2, 14)}[fmt]
    v = np.moveaxis(np.asarray(x, np.float32).astype(ml_dtypes.bfloat16).astype(np.float64), axis, -1)
    blocks = v.reshape(v.shape[:-1] + (-1, 32))
    amax = np.abs(blocks).max(-1, keepdims=True)
    byte = np.maximum(np.where(amax > 0, np.frexp(amax)[1] - 1 + 127, 0) - down, 1)
    scale = np.exp2(byte - 127.0)
    codes = (blocks / scale).astype(np.float32).astype(dtype).astype(np.float64)
    return np.moveaxis((codes * scale).reshape(v.shape), -1, axis)


WIDE = False


def mx_kscale(k):
    if not WIDE:
        return np.ones(k)
    levels = np.array([10, -10, 5, -5, 0])
    if k % 512:
        return np.exp2(np.random.permutation(np.resize(levels, k // 32))).repeat(32)
    a = np.empty((k // 512, 16))
    for p in range(k // 512):
        a[p, :8] = np.random.permutation(np.resize(levels, 8))
        for g in range(8):
            far = levels[np.abs(levels - a[p, g]) >= 10]
            a[p, g + 8] = far[np.random.randint(len(far))]
    return np.exp2(a.ravel()).repeat(32)


def f64(x):
    return np.asarray(x).astype(np.float64)


def striped(idx):
    return np.tile(idx.reshape(-1, 16).T, (8, 1)).astype(np.uint16)


def unstriped(offs):
    return offs[:16].T.reshape(-1).astype(np.int64)


E2M1 = np.array([0.0, 0.5, 1.0, 1.5, 2.0, 3.0, 4.0, 6.0, -0.0, -0.5, -1.0, -1.5, -2.0, -3.0, -4.0, -6.0])


def pack_weight(w, fmt):
    k, n = w.shape
    w = f64(np.asarray(w, np.float32).astype(ml_dtypes.bfloat16)).reshape(k // 32, 32, n)
    amax = np.abs(w).max(1)
    if fmt == "e4m3":
        byte = np.frexp(amax)[1] - 1 + 127 - 7
    else:
        mant, ex = np.frexp(amax / 6.0)
        byte = np.where(mant > 0.5, ex, ex - 1) + 127
    byte = np.clip(np.where(amax > 0, byte, 1), 1, 254)
    scaled = (w * np.exp2(127.0 - byte)[:, None, :]).reshape(k, n).astype(np.float32)
    by_word = np.ascontiguousarray(scaled.reshape(k // 512, 128, 4, n).transpose(0, 1, 3, 2))
    if fmt == "e4m3":
        words = by_word.astype(ml_dtypes.float8_e4m3fn).view(np.uint8)
    else:
        c = by_word.astype(ml_dtypes.float4_e2m1fn).view(np.uint8) & 0xF
        words = (c[..., 0::2] | (c[..., 1::2] << 4)).reshape(k // 512, 128, 2 * n)
    return np.ascontiguousarray(words), np.ascontiguousarray(byte.astype(np.uint8).reshape(k // 512, 16, n))


def unpack_weight(words, scales, fmt):
    g, _, n = scales.shape
    words = np.ascontiguousarray(words).reshape(g, 128, n, -1)
    if fmt == "e4m3":
        vals = words.view(ml_dtypes.float8_e4m3fn).astype(np.float64)
    else:
        nib = np.empty((g, 128, n, 4), np.uint8)
        nib[..., 0::2] = words & 0xF
        nib[..., 1::2] = words >> 4
        vals = E2M1[nib]
    vals = vals * np.repeat(np.exp2(scales.astype(np.float64) - 127.0), 8, axis=1)[..., None]
    return vals.transpose(0, 1, 3, 2).reshape(g * 512, n)


def gelu(v):
    return 0.5 * v * (1.0 + np.tanh(np.sqrt(2.0 / np.pi) * (v + 0.044715 * v**3)))


def twice(P):
    return np.random.permutation(np.repeat(np.arange(P), 2))


K, H, T, S, P = 1024, 512, 4096, 1024, 512


def setup_inputs():
    n = np.random.standard_normal
    s = mx_kscale(K)[:, None]
    u = mx_kscale(H)[:, None]
    d = {}
    d["tab_words"], d["tab_scales"] = pack_weight(n((K, T)) * s, "e4m3")
    d["offs"] = striped(np.random.permutation(T)[:S])
    d["pos1"] = striped(np.random.permutation(S)[:P])
    d["pos2"] = striped(np.random.permutation(S)[:P])
    d["pos3"] = striped(twice(P))
    d["w1"] = (0.56 * n((K, H)) / K**0.5 / s).astype(np.float32)
    sign = np.where(n(H) > 0, 1.0, -1.0)
    d["gain"] = (sign * np.random.uniform(0.6, 1.4, H) * u[:, 0]).astype(np.float32)
    d["w2"] = (n((H, H)) / H**0.5 / u * u.T).astype(np.float32)
    d["w3_words"], d["w3_scales"] = pack_weight(n((H, H)) / H**0.5 / u * u.T, "e2m1")
    d["span"] = (np.random.uniform(0.6, 1.6, H) * u[:, 0]).astype(np.float32)
    return d


def reference(tab_words, tab_scales, offs, pos1, pos2, pos3, w1, gain, w2, w3_words, w3_scales, span):
    v = unpack_weight(tab_words, tab_scales, "e4m3")[:, unstriped(offs)]
    f = f64(gain)[:, None] * np.cos(mxq(f64(w1), 0, "e4m3").T @ v)
    h = (mxq(f64(w2), 0, "e4m3").T @ mxq(f, 0, "e4m3")) - f
    pair = h[:, unstriped(pos1)] + h[:, unstriped(pos2)]
    w3 = unpack_weight(w3_words, w3_scales, "e2m1")
    y = w3.T @ mxq(pair, 0, "e4m3")
    return y[:, unstriped(pos3)] / (f64(span)[:, None] + np.abs(h))

@@ -1,0 +1,268 @@
+import math
+from contextlib import ExitStack
+
+import concourse.mybir as mybir
+
+K, H, T, S, NP = 1024, 512, 4096, 1024, 512
+FLOPS = 2 * (K * H * S + H * H * S + H * H * NP)
+
+F32 = mybir.dt.float32
+BF16 = mybir.dt.bfloat16
+I32 = mybir.dt.int32
+U32 = mybir.dt.uint32
+U16 = mybir.dt.uint16
+U8 = mybir.dt.uint8
+FP8X4 = mybir.dt.float8_e4m3fn_x4
+FP4X4 = mybir.dt.float4_e2m1fn_x4
+ALU = mybir.AluOpType
+ACT = mybir.ActivationFunctionType
+
+P = 128
+PACK = 4
+HALF = 512
+PH = 256
+SPARE = 32
+TWO_PI = 2.0 * math.pi
+
+
+def tile_list_iris_sector_matcher_kernel(
+    tc, tab_words, tab_scales, offs, pos1, pos2, pos3, w1, gain, w2, w3_words, w3_scales, span, out
+):
+    nc = tc.nc
+    with ExitStack() as ctx:
+        lists = ctx.enter_context(tc.tile_pool(name="lists", bufs=1))
+        keep = ctx.enter_context(tc.tile_pool(name="keep", bufs=1))
+        ring = ctx.enter_context(tc.tile_pool(name="ring", bufs=3))
+        psum = ctx.enter_context(tc.psum_pool(name="psum", bufs=8))
+
+        def held(name, shape, dtype, after=None):
+            return keep.tile(shape, dtype, name=name, tag=after or name, align_bytes=64)
+
+        offs_sb = lists.tile([P, S // 16], U16, name="offs_sb")
+        pos1_sb = lists.tile([P, NP // 16], U16, name="pos1_sb")
+        pos2_sb = lists.tile([P, NP // 16], U16, name="pos2_sb")
+        pos3_sb = lists.tile([P, S // 16], U16, name="pos3_sb")
+
+        warm = held("warm", [P, 2], F32)
+        nc.gpsimd.memset(warm[:, 0:1], 0.0)
+        nc.scalar.activation(warm[:, 1:2], warm[:, 0:1], ACT.Sin)
+
+        tab_sc = held("tab_sc", [P, T // 4], I32)
+        nc.vector.memset(tab_sc[:], 0)
+        w3_sc_raw = held("w3_sc_raw", [P, H // 4], I32)
+        nc.gpsimd.memset(w3_sc_raw[:], 0)
+
+        table = [held("table%d" % a, [P, T], I32) for a in range(2)]
+        w1_rows = [w1[512 * a : 512 * (a + 1), :].rearrange("(p j) c -> p j c", j=PACK) for a in range(2)]
+        w1_raw0 = held("w1_raw0", [P, PACK, H], F32)
+        w1_raw1 = [held("w1_raw1_%d" % u, [P, PACK, H // 2], F32) for u in range(2)]
+        w2_raw = held("w2_raw", [P, PACK, H], F32)
+        gain_sb = held("gain_sb", [P, PACK], F32)
+        span_sb = held("span_sb", [P, PACK], F32)
+        w3_raw = held("w3_raw", [P, 2 * H // 4], I32)
+
+        def table_words(a):
+            return tab_words[a].rearrange("p n i -> p (n i)").bitcast(I32)
+
+        nc.sync.dma_start(offs_sb[:], offs)
+        nc.sync.dma_start(table[0][:], table_words(0))
+        for q in range(4):
+            nc.sync.dma_start(tab_sc[32 * q : 32 * q + 8, :], tab_scales[:, 4 * q : 4 * q + 4, :].bitcast(I32))
+        nc.sync.dma_start(w1_raw0[:], w1_rows[0])
+        nc.sync.dma_start(table[1][:], table_words(1))
+        for u in range(2):
+            nc.sync.dma_start(w1_raw1[u][:], w1_rows[1][:, :, 256 * u : 256 * (u + 1)])
+        nc.sync.dma_start(w2_raw[:], w2.rearrange("(p j) c -> p j c", j=PACK))
+        nc.sync.dma_start(pos1_sb[:], pos1)
+        nc.sync.dma_start(pos2_sb[:], pos2)
+        nc.sync.dma_start(pos3_sb[:], pos3)
+        nc.scalar.dma_start(gain_sb[:], gain.rearrange("(p t) -> p t", t=PACK))
+        nc.scalar.dma_start(span_sb[:], span.rearrange("(p t) -> p t", t=PACK))
+        nc.gpsimd.dma_start(w3_raw[:], w3_words[0].bitcast(I32))
+        for q in range(4):
+            nc.gpsimd.dma_start(w3_sc_raw[32 * q : 32 * q + 4, :], w3_scales[0, 4 * q : 4 * q + 4, :].bitcast(I32))
+
+        y = [held("y%d" % t, [P, NP + SPARE], F32) for t in range(PACK)]
+        for t in range(PACK):
+            nc.gpsimd.memset(y[t][:, NP:], 0.0)
+        neg_gain = held("neg_gain", [P, PACK], F32)
+        nc.vector.tensor_scalar(neg_gain[:], gain_sb[:], -1.0, None, ALU.mult)
+
+        def dealt(grouped):
+            return grouped[:].rearrange("p (t m j) -> p m j t", t=PACK, j=PACK)
+
+        def by_column(raw):
+            return raw[:].rearrange("p j (m t) -> p m j t", t=PACK)
+
+        def quantise(codes, scales, values):
+            nc.vector.quantize_mx(out=codes.bitcast(FP8X4), scales=scales, in_=values)
+
+        v_words = [held("v_words%d" % a, [P, S], U32) for a in range(2)]
+        v_sc = held("v_sc", [P, S], U8)
+        w1_bf = [held("w1_bf%d" % a, [P, PACK * H], BF16) for a in range(2)]
+        w1_q = [held("w1_q%d" % a, [P, H], U32) for a in range(2)]
+        w1_sc = [held("w1_sc%d" % a, [P, H], U8) for a in range(2)]
+
+        nc.vector.tensor_copy(v_words[0][:], table[0][:].bitcast(U32).indirect(offs_sb[:]))
+        nc.vector.tensor_copy(v_sc[:], tab_sc[:].bitcast(U8).indirect(offs_sb[:]))
+        nc.scalar.copy(dealt(w1_bf[0]), by_column(w1_raw0))
+        quantise(w1_q[0][:], w1_sc[0][:], w1_bf[0][:])
+        for u in range(2):
+            nc.vector.tensor_copy(
+                v_words[1][:, HALF * u : HALF * (u + 1)],
+                table[1][:].bitcast(U32).indirect(offs_sb[:, 32 * u : 32 * (u + 1)]),
+            )
+        nc.scalar.copy(dealt(w1_bf[1])[:, 0:64], by_column(w1_raw1[0]))
+        nc.vector.tensor_copy(dealt(w1_bf[1])[:, 64:128], by_column(w1_raw1[1]))
+        for u in range(2):
+            quantise(
+                w1_q[1][:, 256 * u : 256 * (u + 1)],
+                w1_sc[1][:, 256 * u : 256 * (u + 1)],
+                w1_bf[1][:, 1024 * u : 1024 * (u + 1)],
+            )
+
+        z = {}
+        for a in range(2):
+            for u in range(2):
+                cols = slice(HALF * u, HALF * (u + 1))
+                for t in range(PACK):
+                    if a == 0:
+                        z[u, t] = psum.tile([P, HALF], F32, name="bank")
+                    rows = slice(P * t, P * (t + 1))
+                    nc.tensor.matmul_mx(
+                        out=z[u, t][:],
+                        lhsT=w1_q[a][:, rows].bitcast(FP8X4),
+                        lhsT_scale=w1_sc[a][:, rows],
+                        rhs=v_words[a][:, cols].bitcast(FP8X4),
+                        rhs_scale=v_sc[4 * a : P, cols],
+                        start=(a == 0),
+                        stop=(a == 1),
+                    )
+
+        cosine = [held("cosine%d" % u, [P, PACK, HALF], F32) for u in range(2)]
+        f_bf = [held("f_bf%d" % u, [P, PACK * HALF], BF16) for u in range(2)]
+        f_q = [held("f_q%d" % u, [P, HALF], U32) for u in range(2)]
+        f_sc = [held("f_sc%d" % u, [P, HALF], U8) for u in range(2)]
+        h = [held("h%d" % t, [P, S], F32) for t in range(PACK)]
+        damp = [held("damp%d" % t, [P, S], F32) for t in range(PACK)]
+
+        def cosines(u, t, on_vector):
+            turns = ring.tile([P, HALF], I32, name="turns")
+            rest = ring.tile([P, HALF], F32, name="rest")
+            if on_vector:
+                angle = z[u, t]
+                nc.vector.tensor_scalar(turns[:], angle[:], 1.0 / TWO_PI, -0.25, ALU.mult, ALU.add)
+            else:
+                angle = ring.tile([P, HALF], F32, name="angle")
+                nc.scalar.activation(angle[:], z[u, t][:], ACT.Abs)
+                nc.scalar.activation(turns[:].bitcast(U32), angle[:], ACT.Copy, bias=-0.25, scale=1.0 / TWO_PI)
+            nc.vector.scalar_tensor_tensor(rest[:], turns[:], -TWO_PI, angle[:], ALU.mult, ALU.add)
+            nc.scalar.activation(cosine[u][:, t, :], rest[:], ACT.Sin, bias=math.pi / 2, scale=-1.0)
+
+        def woven(tile):
+            return tile[:].rearrange("p (c i t) -> p c t i", i=4, t=PACK)
+
+        def by_fours(tile):
+            return tile[:].rearrange("p t (c i) -> p c t i", i=4)
+
+        def features(u):
+            gains = gain_sb[:].unsqueeze(1).unsqueeze(3).to_broadcast([P, HALF // 4, PACK, 4])
+            nc.vector.tensor_tensor(woven(f_bf[u]), by_fours(cosine[u]), gains, ALU.mult)
+            quantise(f_q[u][:], f_sc[u][:], f_bf[u][:])
+
+        w2_bf = held("w2_bf", [P, PACK * H], BF16)
+        w2_q = held("w2_q", [P, H], U32)
+        w2_sc = held("w2_sc", [P, H], U8)
+
+        def second(u):
+            cols = slice(HALF * u, HALF * (u + 1))
+            for t in range(PACK):
+                rows = slice(P * t, P * (t + 1))
+                acc = psum.tile([P, HALF], F32, name="bank")
+                nc.tensor.matmul_mx(
+                    out=acc[:],
+                    lhsT=w2_q[:, rows].bitcast(FP8X4),
+                    lhsT_scale=w2_sc[:, rows],
+                    rhs=f_q[u][:].bitcast(FP8X4),
+                    rhs_scale=f_sc[u][:],
+                    start=True,
+                    stop=True,
+                )
+                nc.vector.scalar_tensor_tensor(
+                    h[t][:, cols], cosine[u][:, t, :], neg_gain[:, t : t + 1], acc[:], ALU.mult, ALU.add
+                )
+            for t in range(PACK):
+                nc.scalar.activation(damp[t][:, cols], h[t][:, cols], ACT.Abs)
+
+        for t in range(PACK):
+            cosines(0, t, on_vector=(t % 2 == 0))
+        nc.scalar.copy(dealt(w2_bf), by_column(w2_raw))
+        features(0)
+        quantise(w2_q[:], w2_sc[:], w2_bf[:])
+        for t in range(PACK):
+            cosines(1, t, on_vector=False)
+        second(0)
+        features(1)
+        second(1)
+
+        def damping(t):
+            root = ring.tile([P, S], F32, name="root", bufs=2)
+            nc.scalar.activation(root[:], damp[t][:], ACT.Abs_reciprocal_sqrt, bias=span_sb[:, t : t + 1])
+            nc.scalar.activation(damp[t][:], root[:], ACT.Square)
+
+        w3_q = held("w3_q", [P, 2 * H], U8, after="w1_bf1")
+        w3_sc = held("w3_sc", [P, H], U8, after="w1_raw1_1")
+        nc.vector.tensor_copy(
+            w3_q[:].rearrange("p (t m b) -> p m t b", t=PACK, b=2),
+            w3_raw[:].bitcast(U8).rearrange("p (m t b) -> p m t b", t=PACK, b=2),
+        )
+        nc.vector.tensor_copy(
+            w3_sc[:].rearrange("p (t m) -> p m t", t=PACK),
+            w3_sc_raw[:].bitcast(U8).rearrange("p (m t) -> p m t", t=PACK),
+        )
+
+        def third(u):
+            entries = slice(PH // 16 * u, PH // 16 * (u + 1))
+            pair = held("pair%d" % u, [P, PACK, PH], F32)
+            pair_bf = held("pair_bf%d" % u, [P, PACK * PH], BF16)
+            pair_q = held("pair_q%d" % u, [P, PH], U32)
+            pair_sc = held("pair_sc%d" % u, [P, PH], U8)
+            first = {}
+            for step in range(PACK + 1):
+                if step < PACK:
+                    first[step] = ring.tile([P, PH], F32, name="first")
+                    nc.vector.tensor_copy(first[step][:], h[step][:].indirect(pos1_sb[:, entries]))
+                if step > 0:
+                    t = step - 1
+                    nc.vector.tensor_tensor(pair[:, t, :], h[t][:].indirect(pos2_sb[:, entries]), first[t][:], ALU.add)
+            nc.vector.tensor_copy(woven(pair_bf), by_fours(pair))
+            quantise(pair_q[:], pair_sc[:], pair_bf[:])
+            for t in range(PACK):
+                acc = psum.tile([P, PH], F32, name="bank")
+                nc.tensor.matmul_mx(
+                    out=acc[:],
+                    lhsT=w3_q[:, 2 * P * t : 2 * P * (t + 1)].bitcast(FP4X4),
+                    lhsT_scale=w3_sc[:, P * t : P * (t + 1)],
+                    rhs=pair_q[:].bitcast(FP8X4),
+                    rhs_scale=pair_sc[:],
+                    start=True,
+                    stop=True,
+                )
+                nc.scalar.copy(y[t][:, PH * u : PH * (u + 1)], acc[:])
+
+        damping(0)
+        damping(1)
+        third(0)
+        damping(2)
+        third(1)
+        damping(3)
+
+        out_rows = out.rearrange("(p t) j -> p t j", t=PACK)
+        for t in range(PACK):
+            for u in range(2):
+                cols = slice(HALF * u, HALF * (u + 1))
+                result = ring.tile([P, HALF], F32, name="result", bufs=4)
+                nc.vector.tensor_tensor(
+                    result[:], y[t][:].indirect(pos3_sb[:, 32 * u : 32 * (u + 1)]), damp[t][:, cols], ALU.mult
+                )
+                nc.sync.dma_start(out_rows[:, t, cols], result[:])

@@ -66,8 +66,6 @@ def tile_list_iris_sector_matcher_kernel(
 
         nc.sync.dma_start(offs_sb[:], offs)
         nc.sync.dma_start(table[0][:], table_words(0))
-        for q in range(4):
-            nc.sync.dma_start(tab_sc[32 * q : 32 * q + 8, :], tab_scales[:, 4 * q : 4 * q + 4, :].bitcast(I32))
         nc.sync.dma_start(w1_raw0[:], w1_rows[0])
         nc.sync.dma_start(table[1][:], table_words(1))
         for u in range(2):
@@ -78,6 +76,8 @@ def tile_list_iris_sector_matcher_kernel(
         nc.sync.dma_start(pos3_sb[:], pos3)
         nc.scalar.dma_start(gain_sb[:], gain.rearrange("(p t) -> p t", t=PACK))
         nc.scalar.dma_start(span_sb[:], span.rearrange("(p t) -> p t", t=PACK))
+        for q in range(4):
+            nc.gpsimd.dma_start(tab_sc[32 * q : 32 * q + 8, :], tab_scales[:, 4 * q : 4 * q + 4, :].bitcast(I32))
         nc.gpsimd.dma_start(w3_raw[:], w3_words[0].bitcast(I32))
         for q in range(4):
             nc.gpsimd.dma_start(w3_sc_raw[32 * q : 32 * q + 4, :], w3_scales[0, 4 * q : 4 * q + 4, :].bitcast(I32))
@@ -98,7 +98,7 @@ def tile_list_iris_sector_matcher_kernel(
             nc.vector.quantize_mx(out=codes.bitcast(FP8X4), scales=scales, in_=values)
 
         v_words = [held("v_words%d" % a, [P, S], U32) for a in range(2)]
-        v_sc = held("v_sc", [P, S], U8)
+        v_sc = held("v_sc", [P, S], U8, after="table0")
         w1_bf = [held("w1_bf%d" % a, [P, PACK * H], BF16) for a in range(2)]
         w1_q = [held("w1_q%d" % a, [P, H], U32) for a in range(2)]
         w1_sc = [held("w1_sc%d" % a, [P, H], U8) for a in range(2)]
@@ -114,18 +114,14 @@ def tile_list_iris_sector_matcher_kernel(
             )
         nc.scalar.copy(dealt(w1_bf[1])[:, 0:64], by_column(w1_raw1[0]))
         nc.vector.tensor_copy(dealt(w1_bf[1])[:, 64:128], by_column(w1_raw1[1]))
-        for u in range(2):
-            quantise(
-                w1_q[1][:, 256 * u : 256 * (u + 1)],
-                w1_sc[1][:, 256 * u : 256 * (u + 1)],
-                w1_bf[1][:, 1024 * u : 1024 * (u + 1)],
-            )
+        for lo, hi in ((0, P), (P, 2 * P), (2 * P, H)):
+            quantise(w1_q[1][:, lo:hi], w1_sc[1][:, lo:hi], w1_bf[1][:, PACK * lo : PACK * hi])
 
         z = {}
         for a in range(2):
-            for u in range(2):
-                cols = slice(HALF * u, HALF * (u + 1))
-                for t in range(PACK):
+            for t in range(PACK):
+                for u in range(2):
+                    cols = slice(HALF * u, HALF * (u + 1))
                     if a == 0:
                         z[u, t] = psum.tile([P, HALF], F32, name="bank")
                     rows = slice(P * t, P * (t + 1))
@@ -146,18 +142,26 @@ def tile_list_iris_sector_matcher_kernel(
         h = [held("h%d" % t, [P, S], F32) for t in range(PACK)]
         damp = [held("damp%d" % t, [P, S], F32) for t in range(PACK)]
 
-        def cosines(u, t, on_vector):
-            turns = ring.tile([P, HALF], I32, name="turns")
-            rest = ring.tile([P, HALF], F32, name="rest")
-            if on_vector:
-                angle = z[u, t]
-                nc.vector.tensor_scalar(turns[:], angle[:], 1.0 / TWO_PI, -0.25, ALU.mult, ALU.add)
+        turns, angle, rest = {}, {}, {}
+
+        def count_turns(u, t):
+            turns[u, t] = ring.tile([P, HALF], I32, name="turns", bufs=4)
+            if u == 0:
+                angle[u, t] = z[u, t]
+                nc.vector.tensor_scalar(turns[u, t][:], z[u, t][:], 1.0 / TWO_PI, -0.25, ALU.mult, ALU.add)
             else:
-                angle = ring.tile([P, HALF], F32, name="angle")
-                nc.scalar.activation(angle[:], z[u, t][:], ACT.Abs)
-                nc.scalar.activation(turns[:].bitcast(U32), angle[:], ACT.Copy, bias=-0.25, scale=1.0 / TWO_PI)
-            nc.vector.scalar_tensor_tensor(rest[:], turns[:], -TWO_PI, angle[:], ALU.mult, ALU.add)
-            nc.scalar.activation(cosine[u][:, t, :], rest[:], ACT.Sin, bias=math.pi / 2, scale=-1.0)
+                angle[u, t] = ring.tile([P, HALF], F32, name="angle")
+                nc.scalar.activation(angle[u, t][:], z[u, t][:], ACT.Abs)
+                nc.scalar.activation(
+                    turns[u, t][:].bitcast(U32), angle[u, t][:], ACT.Copy, bias=-0.25, scale=1.0 / TWO_PI
+                )
+
+        def reduce_angle(u, t):
+            rest[u, t] = ring.tile([P, HALF], F32, name="rest", bufs=4)
+            nc.vector.scalar_tensor_tensor(rest[u, t][:], turns[u, t][:], -TWO_PI, angle[u, t][:], ALU.mult, ALU.add)
+
+        def take_cosine(u, t):
+            nc.scalar.activation(cosine[u][:, t, :], rest[u, t][:], ACT.Sin, bias=math.pi / 2, scale=-1.0)
 
         def woven(tile):
             return tile[:].rearrange("p (c i t) -> p c t i", i=4, t=PACK)
@@ -168,19 +172,18 @@ def tile_list_iris_sector_matcher_kernel(
         def features(u):
             gains = gain_sb[:].unsqueeze(1).unsqueeze(3).to_broadcast([P, HALF // 4, PACK, 4])
             nc.vector.tensor_tensor(woven(f_bf[u]), by_fours(cosine[u]), gains, ALU.mult)
-            quantise(f_q[u][:], f_sc[u][:], f_bf[u][:])
 
         w2_bf = held("w2_bf", [P, PACK * H], BF16)
         w2_q = held("w2_q", [P, H], U32)
         w2_sc = held("w2_sc", [P, H], U8)
+        mixed = {}
 
-        def second(u):
-            cols = slice(HALF * u, HALF * (u + 1))
+        def second_product(u):
             for t in range(PACK):
                 rows = slice(P * t, P * (t + 1))
-                acc = psum.tile([P, HALF], F32, name="bank")
+                mixed[u, t] = psum.tile([P, HALF], F32, name="bank")
                 nc.tensor.matmul_mx(
-                    out=acc[:],
+                    out=mixed[u, t][:],
                     lhsT=w2_q[:, rows].bitcast(FP8X4),
                     lhsT_scale=w2_sc[:, rows],
                     rhs=f_q[u][:].bitcast(FP8X4),
@@ -188,30 +191,63 @@ def tile_list_iris_sector_matcher_kernel(
                     start=True,
                     stop=True,
                 )
-                nc.vector.scalar_tensor_tensor(
-                    h[t][:, cols], cosine[u][:, t, :], neg_gain[:, t : t + 1], acc[:], ALU.mult, ALU.add
-                )
-            for t in range(PACK):
-                nc.scalar.activation(damp[t][:, cols], h[t][:, cols], ACT.Abs)
 
+        def subtract_features(u, t):
+            nc.vector.scalar_tensor_tensor(
+                h[t][:, HALF * u : HALF * (u + 1)],
+                cosine[u][:, t, :],
+                neg_gain[:, t : t + 1],
+                mixed[u, t][:],
+                ALU.mult,
+                ALU.add,
+            )
+
+        def damping(u, t):
+            cols = slice(HALF * u, HALF * (u + 1))
+            size = ring.tile([P, HALF], F32, name="size", bufs=2)
+            root = ring.tile([P, HALF], F32, name="root", bufs=2)
+            nc.scalar.activation(size[:], h[t][:, cols], ACT.Abs)
+            nc.scalar.activation(root[:], size[:], ACT.Abs_reciprocal_sqrt, bias=span_sb[:, t : t + 1])
+            nc.scalar.activation(damp[t][:, cols], root[:], ACT.Square)
+
+        count_turns(0, 0)
+        count_turns(1, 0)
         for t in range(PACK):
-            cosines(0, t, on_vector=(t % 2 == 0))
-        nc.scalar.copy(dealt(w2_bf), by_column(w2_raw))
+            if t + 1 < PACK:
+                count_turns(0, t + 1)
+            reduce_angle(0, t)
+            take_cosine(0, t)
+            if t == 0:
+                count_turns(1, 1)
+        reduce_angle(1, 0)
         features(0)
+        for piece in range(4):
+            nc.scalar.copy(
+                dealt(w2_bf)[:, 32 * piece : 32 * (piece + 1)], by_column(w2_raw)[:, 32 * piece : 32 * (piece + 1)]
+            )
+        reduce_angle(1, 1)
+        quantise(f_q[0][:], f_sc[0][:], f_bf[0][:])
         quantise(w2_q[:], w2_sc[:], w2_bf[:])
+        second_product(0)
+        for t in (2, 3):
+            count_turns(1, t)
+            reduce_angle(1, t)
         for t in range(PACK):
-            cosines(1, t, on_vector=False)
-        second(0)
+            take_cosine(1, t)
+        subtract_features(0, 0)
         features(1)
-        second(1)
+        subtract_features(0, 1)
+        quantise(f_q[1][:], f_sc[1][:], f_bf[1][:])
+        second_product(1)
+        subtract_features(0, 2)
+        subtract_features(0, 3)
+        for t in range(PACK):
+            damping(0, t)
+        for t in range(PACK):
+            subtract_features(1, t)
 
-        def damping(t):
-            root = ring.tile([P, S], F32, name="root", bufs=2)
-            nc.scalar.activation(root[:], damp[t][:], ACT.Abs_reciprocal_sqrt, bias=span_sb[:, t : t + 1])
-            nc.scalar.activation(damp[t][:], root[:], ACT.Square)
-
-        w3_q = held("w3_q", [P, 2 * H], U8, after="w1_bf1")
-        w3_sc = held("w3_sc", [P, H], U8, after="w1_raw1_1")
+        w3_q = held("w3_q", [P, 2 * H], U8, after="w1_bf0")
+        w3_sc = held("w3_sc", [P, H], U8, after="tab_sc")
         nc.vector.tensor_copy(
             w3_q[:].rearrange("p (t m b) -> p m t b", t=PACK, b=2),
             w3_raw[:].bitcast(U8).rearrange("p (m t b) -> p m t b", t=PACK, b=2),
@@ -230,12 +266,18 @@ def tile_list_iris_sector_matcher_kernel(
             first = {}
             for step in range(PACK + 1):
                 if step < PACK:
-                    first[step] = ring.tile([P, PH], F32, name="first")
+                    if (u, step) == (1, 2):
+                        first[step] = held("first_late", [P, PH], F32, after="pair_bf0")
+                    else:
+                        first[step] = ring.tile([P, PH], F32, name="first")
                     nc.vector.tensor_copy(first[step][:], h[step][:].indirect(pos1_sb[:, entries]))
                 if step > 0:
                     t = step - 1
                     nc.vector.tensor_tensor(pair[:, t, :], h[t][:].indirect(pos2_sb[:, entries]), first[t][:], ALU.add)
-            nc.vector.tensor_copy(woven(pair_bf), by_fours(pair))
+            if u == 0:
+                nc.scalar.copy(woven(pair_bf), by_fours(pair))
+            else:
+                nc.vector.tensor_copy(woven(pair_bf), by_fours(pair))
             quantise(pair_q[:], pair_sc[:], pair_bf[:])
             for t in range(PACK):
                 acc = psum.tile([P, PH], F32, name="bank")
@@ -250,19 +292,19 @@ def tile_list_iris_sector_matcher_kernel(
                 )
                 nc.scalar.copy(y[t][:, PH * u : PH * (u + 1)], acc[:])
 
-        damping(0)
-        damping(1)
+        damping(1, 0)
+        damping(1, 1)
         third(0)
-        damping(2)
         third(1)
-        damping(3)
+        damping(1, 2)
+        damping(1, 3)
 
         out_rows = out.rearrange("(p t) j -> p t j", t=PACK)
         for t in range(PACK):
-            for u in range(2):
-                cols = slice(HALF * u, HALF * (u + 1))
-                result = ring.tile([P, HALF], F32, name="result", bufs=4)
+            edges = (0, HALF, S) if t + 1 < PACK else (0, HALF, S - PH, S)
+            for lo, hi in zip(edges, edges[1:]):
+                result = ring.tile([P, hi - lo], F32, name="result", bufs=4)
                 nc.vector.tensor_tensor(
-                    result[:], y[t][:].indirect(pos3_sb[:, 32 * u : 32 * (u + 1)]), damp[t][:, cols], ALU.mult
+                    result[:], y[t][:].indirect(pos3_sb[:, lo // 16 : hi // 16]), damp[t][:, lo:hi], ALU.mult
                 )
-                nc.sync.dma_start(out_rows[:, t, cols], result[:])
+                nc.sync.dma_start(out_rows[:, t, lo:hi], result[:])

@@ -64,23 +64,29 @@ def tile_list_iris_sector_matcher_kernel(
         def table_words(a):
             return tab_words[a].rearrange("p n i -> p (n i)").bitcast(I32)
 
+        def scale_rows(scales, q):
+            return scales[4 * q : 4 * q + 4, :].bitcast(I32)
+
         nc.sync.dma_start(offs_sb[:], offs)
         nc.sync.dma_start(table[0][:], table_words(0))
+        for q in range(2):
+            for a in range(2):
+                nc.sync.dma_start(tab_sc[32 * q + 4 * a : 32 * q + 4 * a + 4, :], scale_rows(tab_scales[a], q))
+        for q in range(2, 4):
+            nc.sync.dma_start(tab_sc[32 * q : 32 * q + 8, :], tab_scales[:, 4 * q : 4 * q + 4, :].bitcast(I32))
         nc.sync.dma_start(w1_raw0[:], w1_rows[0])
         nc.sync.dma_start(table[1][:], table_words(1))
         for u in range(2):
             nc.sync.dma_start(w1_raw1[u][:], w1_rows[1][:, :, 256 * u : 256 * (u + 1)])
+        nc.sync.dma_start(gain_sb[:], gain.rearrange("(p t) -> p t", t=PACK))
         nc.sync.dma_start(w2_raw[:], w2.rearrange("(p j) c -> p j c", j=PACK))
+        nc.sync.dma_start(span_sb[:], span.rearrange("(p t) -> p t", t=PACK))
+        nc.sync.dma_start(w3_raw[:], w3_words[0].bitcast(I32))
+        for q in range(4):
+            nc.sync.dma_start(w3_sc_raw[32 * q : 32 * q + 4, :], scale_rows(w3_scales[0], q))
         nc.sync.dma_start(pos1_sb[:], pos1)
         nc.sync.dma_start(pos2_sb[:], pos2)
         nc.sync.dma_start(pos3_sb[:], pos3)
-        nc.scalar.dma_start(gain_sb[:], gain.rearrange("(p t) -> p t", t=PACK))
-        nc.scalar.dma_start(span_sb[:], span.rearrange("(p t) -> p t", t=PACK))
-        for q in range(4):
-            nc.gpsimd.dma_start(tab_sc[32 * q : 32 * q + 8, :], tab_scales[:, 4 * q : 4 * q + 4, :].bitcast(I32))
-        nc.gpsimd.dma_start(w3_raw[:], w3_words[0].bitcast(I32))
-        for q in range(4):
-            nc.gpsimd.dma_start(w3_sc_raw[32 * q : 32 * q + 4, :], w3_scales[0, 4 * q : 4 * q + 4, :].bitcast(I32))
 
         y = [held("y%d" % t, [P, NP + SPARE], F32) for t in range(PACK)]
         for t in range(PACK):
@@ -246,8 +252,8 @@ def tile_list_iris_sector_matcher_kernel(
         for t in range(PACK):
             subtract_features(1, t)
 
-        w3_q = held("w3_q", [P, 2 * H], U8, after="w1_bf0")
-        w3_sc = held("w3_sc", [P, H], U8, after="tab_sc")
+        w3_q = held("w3_q", [P, 2 * H], U8, after="f_bf0")
+        w3_sc = held("w3_sc", [P, H], U8, after="w2_bf")
         nc.vector.tensor_copy(
             w3_q[:].rearrange("p (t m b) -> p m t b", t=PACK, b=2),
             w3_raw[:].bitcast(U8).rearrange("p (m t b) -> p m t b", t=PACK, b=2),

@@ -75,15 +75,15 @@ def tile_list_iris_sector_matcher_kernel(
         for q in range(2, 4):
             nc.sync.dma_start(tab_sc[32 * q : 32 * q + 8, :], tab_scales[:, 4 * q : 4 * q + 4, :].bitcast(I32))
         nc.sync.dma_start(w1_raw0[:], w1_rows[0])
+        nc.sync.dma_start(w3_raw[:], w3_words[0].bitcast(I32))
+        for q in range(4):
+            nc.sync.dma_start(w3_sc_raw[32 * q : 32 * q + 4, :], scale_rows(w3_scales[0], q))
         nc.sync.dma_start(table[1][:], table_words(1))
         for u in range(2):
             nc.sync.dma_start(w1_raw1[u][:], w1_rows[1][:, :, 256 * u : 256 * (u + 1)])
         nc.sync.dma_start(gain_sb[:], gain.rearrange("(p t) -> p t", t=PACK))
         nc.sync.dma_start(w2_raw[:], w2.rearrange("(p j) c -> p j c", j=PACK))
         nc.sync.dma_start(span_sb[:], span.rearrange("(p t) -> p t", t=PACK))
-        nc.sync.dma_start(w3_raw[:], w3_words[0].bitcast(I32))
-        for q in range(4):
-            nc.sync.dma_start(w3_sc_raw[32 * q : 32 * q + 4, :], scale_rows(w3_scales[0], q))
         nc.sync.dma_start(pos1_sb[:], pos1)
         nc.sync.dma_start(pos2_sb[:], pos2)
         nc.sync.dma_start(pos3_sb[:], pos3)
@@ -119,7 +119,8 @@ def tile_list_iris_sector_matcher_kernel(
                 table[1][:].bitcast(U32).indirect(offs_sb[:, 32 * u : 32 * (u + 1)]),
             )
         nc.scalar.copy(dealt(w1_bf[1])[:, 0:64], by_column(w1_raw1[0]))
-        nc.vector.tensor_copy(dealt(w1_bf[1])[:, 64:128], by_column(w1_raw1[1]))
+        nc.vector.tensor_copy(dealt(w1_bf[1])[:, 64:108], by_column(w1_raw1[1])[:, 0:44])
+        nc.scalar.copy(dealt(w1_bf[1])[:, 108:128], by_column(w1_raw1[1])[:, 44:64])
         for lo, hi in ((0, P), (P, 2 * P), (2 * P, H)):
             quantise(w1_q[1][:, lo:hi], w1_sc[1][:, lo:hi], w1_bf[1][:, PACK * lo : PACK * hi])
 
@@ -170,13 +171,13 @@ def tile_list_iris_sector_matcher_kernel(
             nc.scalar.activation(cosine[u][:, t, :], rest[u, t][:], ACT.Sin, bias=math.pi / 2, scale=-1.0)
 
         def woven(tile):
-            return tile[:].rearrange("p (c i t) -> p c t i", i=4, t=PACK)
+            return tile[:].rearrange("p (c i t) -> p c t i", i=2, t=PACK)
 
         def by_fours(tile):
-            return tile[:].rearrange("p t (c i) -> p c t i", i=4)
+            return tile[:].rearrange("p t (c i) -> p c t i", i=2)
 
         def features(u):
-            gains = gain_sb[:].unsqueeze(1).unsqueeze(3).to_broadcast([P, HALF // 4, PACK, 4])
+            gains = gain_sb[:].unsqueeze(1).unsqueeze(3).to_broadcast([P, HALF // 2, PACK, 2])
             nc.vector.tensor_tensor(woven(f_bf[u]), by_fours(cosine[u]), gains, ALU.mult)
 
         w2_bf = held("w2_bf", [P, PACK * H], BF16)
@@ -252,8 +253,8 @@ def tile_list_iris_sector_matcher_kernel(
         for t in range(PACK):
             subtract_features(1, t)
 
-        w3_q = held("w3_q", [P, 2 * H], U8, after="f_bf0")
-        w3_sc = held("w3_sc", [P, H], U8, after="w2_bf")
+        w3_q = held("w3_q", [P, 2 * H], U8, after="w1_bf0")
+        w3_sc = held("w3_sc", [P, H], U8, after="tab_sc")
         nc.vector.tensor_copy(
             w3_q[:].rearrange("p (t m b) -> p m t b", t=PACK, b=2),
             w3_raw[:].bitcast(U8).rearrange("p (m t b) -> p m t b", t=PACK, b=2),

import math
from contextlib import ExitStack

import concourse.mybir as mybir

K, H, T, S, NP = 1024, 512, 4096, 1024, 512
FLOPS = 2 * (K * H * S + H * H * S + H * H * NP)

F32 = mybir.dt.float32
BF16 = mybir.dt.bfloat16
I32 = mybir.dt.int32
U32 = mybir.dt.uint32
U16 = mybir.dt.uint16
U8 = mybir.dt.uint8
FP8X4 = mybir.dt.float8_e4m3fn_x4
FP4X4 = mybir.dt.float4_e2m1fn_x4
ALU = mybir.AluOpType
ACT = mybir.ActivationFunctionType

P = 128
PACK = 4
HALF = 512
PH = 256
SPARE = 32
TWO_PI = 2.0 * math.pi


def tile_list_iris_sector_matcher_kernel(
    tc, tab_words, tab_scales, offs, pos1, pos2, pos3, w1, gain, w2, w3_words, w3_scales, span, out
):
    nc = tc.nc
    with ExitStack() as ctx:
        lists = ctx.enter_context(tc.tile_pool(name="lists", bufs=1))
        keep = ctx.enter_context(tc.tile_pool(name="keep", bufs=1))
        ring = ctx.enter_context(tc.tile_pool(name="ring", bufs=3))
        psum = ctx.enter_context(tc.psum_pool(name="psum", bufs=8))

        def held(name, shape, dtype, after=None):
            return keep.tile(shape, dtype, name=name, tag=after or name, align_bytes=64)

        offs_sb = lists.tile([P, S // 16], U16, name="offs_sb")
        pos1_sb = lists.tile([P, NP // 16], U16, name="pos1_sb")
        pos2_sb = lists.tile([P, NP // 16], U16, name="pos2_sb")
        pos3_sb = lists.tile([P, S // 16], U16, name="pos3_sb")

        warm = held("warm", [P, 2], F32)
        nc.gpsimd.memset(warm[:, 0:1], 0.0)
        nc.scalar.activation(warm[:, 1:2], warm[:, 0:1], ACT.Sin)

        tab_sc = held("tab_sc", [P, T // 4], I32)
        nc.vector.memset(tab_sc[:], 0)
        w3_sc_raw = held("w3_sc_raw", [P, H // 4], I32)
        nc.gpsimd.memset(w3_sc_raw[:], 0)

        table = [held("table%d" % a, [P, T], I32) for a in range(2)]
        w1_rows = [w1[512 * a : 512 * (a + 1), :].rearrange("(p j) c -> p j c", j=PACK) for a in range(2)]
        w1_raw0 = held("w1_raw0", [P, PACK, H], F32)
        w1_raw1 = [held("w1_raw1_%d" % u, [P, PACK, H // 2], F32) for u in range(2)]
        w2_raw = held("w2_raw", [P, PACK, H], F32)
        gain_sb = held("gain_sb", [P, PACK], F32)
        span_sb = held("span_sb", [P, PACK], F32)
        w3_raw = held("w3_raw", [P, 2 * H // 4], I32)

        def table_words(a):
            return tab_words[a].rearrange("p n i -> p (n i)").bitcast(I32)

        def scale_rows(scales, q):
            return scales[4 * q : 4 * q + 4, :].bitcast(I32)

        nc.sync.dma_start(offs_sb[:], offs)
        nc.sync.dma_start(table[0][:], table_words(0))
        for q in range(2):
            for a in range(2):
                nc.sync.dma_start(tab_sc[32 * q + 4 * a : 32 * q + 4 * a + 4, :], scale_rows(tab_scales[a], q))
        for q in range(2, 4):
            nc.sync.dma_start(tab_sc[32 * q : 32 * q + 8, :], tab_scales[:, 4 * q : 4 * q + 4, :].bitcast(I32))
        nc.sync.dma_start(w1_raw0[:], w1_rows[0])
        nc.sync.dma_start(w3_raw[:], w3_words[0].bitcast(I32))
        for q in range(4):
            nc.sync.dma_start(w3_sc_raw[32 * q : 32 * q + 4, :], scale_rows(w3_scales[0], q))
        nc.sync.dma_start(table[1][:], table_words(1))
        for u in range(2):
            nc.sync.dma_start(w1_raw1[u][:], w1_rows[1][:, :, 256 * u : 256 * (u + 1)])
        nc.sync.dma_start(gain_sb[:], gain.rearrange("(p t) -> p t", t=PACK))
        nc.sync.dma_start(w2_raw[:], w2.rearrange("(p j) c -> p j c", j=PACK))
        nc.sync.dma_start(span_sb[:], span.rearrange("(p t) -> p t", t=PACK))
        nc.sync.dma_start(pos1_sb[:], pos1)
        nc.sync.dma_start(pos2_sb[:], pos2)
        nc.sync.dma_start(pos3_sb[:], pos3)

        y = [held("y%d" % t, [P, NP + SPARE], F32) for t in range(PACK)]
        for t in range(PACK):
            nc.gpsimd.memset(y[t][:, NP:], 0.0)
        neg_gain = held("neg_gain", [P, PACK], F32)
        nc.vector.tensor_scalar(neg_gain[:], gain_sb[:], -1.0, None, ALU.mult)

        def dealt(grouped):
            return grouped[:].rearrange("p (t m j) -> p m j t", t=PACK, j=PACK)

        def by_column(raw):
            return raw[:].rearrange("p j (m t) -> p m j t", t=PACK)

        def quantise(codes, scales, values):
            nc.vector.quantize_mx(out=codes.bitcast(FP8X4), scales=scales, in_=values)

        v_words = [held("v_words%d" % a, [P, S], U32) for a in range(2)]
        v_sc = held("v_sc", [P, S], U8, after="table0")
        w1_bf = [held("w1_bf%d" % a, [P, PACK * H], BF16) for a in range(2)]
        w1_q = [held("w1_q%d" % a, [P, H], U32) for a in range(2)]
        w1_sc = [held("w1_sc%d" % a, [P, H], U8) for a in range(2)]

        nc.vector.tensor_copy(v_words[0][:], table[0][:].bitcast(U32).indirect(offs_sb[:]))
        nc.vector.tensor_copy(v_sc[:], tab_sc[:].bitcast(U8).indirect(offs_sb[:]))
        nc.scalar.copy(dealt(w1_bf[0]), by_column(w1_raw0))
        quantise(w1_q[0][:], w1_sc[0][:], w1_bf[0][:])
        for u in range(2):
            nc.vector.tensor_copy(
                v_words[1][:, HALF * u : HALF * (u + 1)],
                table[1][:].bitcast(U32).indirect(offs_sb[:, 32 * u : 32 * (u + 1)]),
            )
        nc.scalar.copy(dealt(w1_bf[1])[:, 0:64], by_column(w1_raw1[0]))
        nc.vector.tensor_copy(dealt(w1_bf[1])[:, 64:108], by_column(w1_raw1[1])[:, 0:44])
        nc.scalar.copy(dealt(w1_bf[1])[:, 108:128], by_column(w1_raw1[1])[:, 44:64])
        for lo, hi in ((0, P), (P, 2 * P), (2 * P, H)):
            quantise(w1_q[1][:, lo:hi], w1_sc[1][:, lo:hi], w1_bf[1][:, PACK * lo : PACK * hi])

        z = {}
        for a in range(2):
            for t in range(PACK):
                for u in range(2):
                    cols = slice(HALF * u, HALF * (u + 1))
                    if a == 0:
                        z[u, t] = psum.tile([P, HALF], F32, name="bank")
                    rows = slice(P * t, P * (t + 1))
                    nc.tensor.matmul_mx(
                        out=z[u, t][:],
                        lhsT=w1_q[a][:, rows].bitcast(FP8X4),
                        lhsT_scale=w1_sc[a][:, rows],
                        rhs=v_words[a][:, cols].bitcast(FP8X4),
                        rhs_scale=v_sc[4 * a : P, cols],
                        start=(a == 0),
                        stop=(a == 1),
                    )

        cosine = [held("cosine%d" % u, [P, PACK, HALF], F32) for u in range(2)]
        f_bf = [held("f_bf%d" % u, [P, PACK * HALF], BF16) for u in range(2)]
        f_q = [held("f_q%d" % u, [P, HALF], U32) for u in range(2)]
        f_sc = [held("f_sc%d" % u, [P, HALF], U8) for u in range(2)]
        h = [held("h%d" % t, [P, S], F32) for t in range(PACK)]
        damp = [held("damp%d" % t, [P, S], F32) for t in range(PACK)]

        turns, angle, rest = {}, {}, {}

        def count_turns(u, t):
            turns[u, t] = ring.tile([P, HALF], I32, name="turns", bufs=4)
            if u == 0:
                angle[u, t] = z[u, t]
                nc.vector.tensor_scalar(turns[u, t][:], z[u, t][:], 1.0 / TWO_PI, -0.25, ALU.mult, ALU.add)
            else:
                angle[u, t] = ring.tile([P, HALF], F32, name="angle")
                nc.scalar.activation(angle[u, t][:], z[u, t][:], ACT.Abs)
                nc.scalar.activation(
                    turns[u, t][:].bitcast(U32), angle[u, t][:], ACT.Copy, bias=-0.25, scale=1.0 / TWO_PI
                )

        def reduce_angle(u, t):
            rest[u, t] = ring.tile([P, HALF], F32, name="rest", bufs=4)
            nc.vector.scalar_tensor_tensor(rest[u, t][:], turns[u, t][:], -TWO_PI, angle[u, t][:], ALU.mult, ALU.add)

        def take_cosine(u, t):
            nc.scalar.activation(cosine[u][:, t, :], rest[u, t][:], ACT.Sin, bias=math.pi / 2, scale=-1.0)

        def woven(tile):
            return tile[:].rearrange("p (c i t) -> p c t i", i=2, t=PACK)

        def by_fours(tile):
            return tile[:].rearrange("p t (c i) -> p c t i", i=2)

        def features(u):
            gains = gain_sb[:].unsqueeze(1).unsqueeze(3).to_broadcast([P, HALF // 2, PACK, 2])
            nc.vector.tensor_tensor(woven(f_bf[u]), by_fours(cosine[u]), gains, ALU.mult)

        w2_bf = held("w2_bf", [P, PACK * H], BF16)
        w2_q = held("w2_q", [P, H], U32)
        w2_sc = held("w2_sc", [P, H], U8)
        mixed = {}

        def second_product(u):
            for t in range(PACK):
                rows = slice(P * t, P * (t + 1))
                mixed[u, t] = psum.tile([P, HALF], F32, name="bank")
                nc.tensor.matmul_mx(
                    out=mixed[u, t][:],
                    lhsT=w2_q[:, rows].bitcast(FP8X4),
                    lhsT_scale=w2_sc[:, rows],
                    rhs=f_q[u][:].bitcast(FP8X4),
                    rhs_scale=f_sc[u][:],
                    start=True,
                    stop=True,
                )

        def subtract_features(u, t):
            nc.vector.scalar_tensor_tensor(
                h[t][:, HALF * u : HALF * (u + 1)],
                cosine[u][:, t, :],
                neg_gain[:, t : t + 1],
                mixed[u, t][:],
                ALU.mult,
                ALU.add,
            )

        def damping(u, t):
            cols = slice(HALF * u, HALF * (u + 1))
            size = ring.tile([P, HALF], F32, name="size", bufs=2)
            root = ring.tile([P, HALF], F32, name="root", bufs=2)
            nc.scalar.activation(size[:], h[t][:, cols], ACT.Abs)
            nc.scalar.activation(root[:], size[:], ACT.Abs_reciprocal_sqrt, bias=span_sb[:, t : t + 1])
            nc.scalar.activation(damp[t][:, cols], root[:], ACT.Square)

        count_turns(0, 0)
        count_turns(1, 0)
        for t in range(PACK):
            if t + 1 < PACK:
                count_turns(0, t + 1)
            reduce_angle(0, t)
            take_cosine(0, t)
            if t == 0:
                count_turns(1, 1)
        reduce_angle(1, 0)
        features(0)
        for piece in range(4):
            nc.scalar.copy(
                dealt(w2_bf)[:, 32 * piece : 32 * (piece + 1)], by_column(w2_raw)[:, 32 * piece : 32 * (piece + 1)]
            )
        reduce_angle(1, 1)
        quantise(f_q[0][:], f_sc[0][:], f_bf[0][:])
        quantise(w2_q[:], w2_sc[:], w2_bf[:])
        second_product(0)
        for t in (2, 3):
            count_turns(1, t)
            reduce_angle(1, t)
        for t in range(PACK):
            take_cosine(1, t)
        subtract_features(0, 0)
        features(1)
        subtract_features(0, 1)
        quantise(f_q[1][:], f_sc[1][:], f_bf[1][:])
        second_product(1)
        subtract_features(0, 2)
        subtract_features(0, 3)
        for t in range(PACK):
            damping(0, t)
        for t in range(PACK):
            subtract_features(1, t)

        w3_q = held("w3_q", [P, 2 * H], U8, after="w1_bf0")
        w3_sc = held("w3_sc", [P, H], U8, after="tab_sc")
        nc.vector.tensor_copy(
            w3_q[:].rearrange("p (t m b) -> p m t b", t=PACK, b=2),
            w3_raw[:].bitcast(U8).rearrange("p (m t b) -> p m t b", t=PACK, b=2),
        )
        nc.vector.tensor_copy(
            w3_sc[:].rearrange("p (t m) -> p m t", t=PACK),
            w3_sc_raw[:].bitcast(U8).rearrange("p (m t) -> p m t", t=PACK),
        )

        def third(u):
            entries = slice(PH // 16 * u, PH // 16 * (u + 1))
            pair = held("pair%d" % u, [P, PACK, PH], F32)
            pair_bf = held("pair_bf%d" % u, [P, PACK * PH], BF16)
            pair_q = held("pair_q%d" % u, [P, PH], U32)
            pair_sc = held("pair_sc%d" % u, [P, PH], U8)
            first = {}
            for step in range(PACK + 1):
                if step < PACK:
                    if (u, step) == (1, 2):
                        first[step] = held("first_late", [P, PH], F32, after="pair_bf0")
                    else:
                        first[step] = ring.tile([P, PH], F32, name="first")
                    nc.vector.tensor_copy(first[step][:], h[step][:].indirect(pos1_sb[:, entries]))
                if step > 0:
                    t = step - 1
                    nc.vector.tensor_tensor(pair[:, t, :], h[t][:].indirect(pos2_sb[:, entries]), first[t][:], ALU.add)
            if u == 0:
                nc.scalar.copy(woven(pair_bf), by_fours(pair))
            else:
                nc.vector.tensor_copy(woven(pair_bf), by_fours(pair))
            quantise(pair_q[:], pair_sc[:], pair_bf[:])
            for t in range(PACK):
                acc = psum.tile([P, PH], F32, name="bank")
                nc.tensor.matmul_mx(
                    out=acc[:],
                    lhsT=w3_q[:, 2 * P * t : 2 * P * (t + 1)].bitcast(FP4X4),
                    lhsT_scale=w3_sc[:, P * t : P * (t + 1)],
                    rhs=pair_q[:].bitcast(FP8X4),
                    rhs_scale=pair_sc[:],
                    start=True,
                    stop=True,
                )
                nc.scalar.copy(y[t][:, PH * u : PH * (u + 1)], acc[:])

        damping(1, 0)
        damping(1, 1)
        third(0)
        third(1)
        damping(1, 2)
        damping(1, 3)

        out_rows = out.rearrange("(p t) j -> p t j", t=PACK)
        for t in range(PACK):
            edges = (0, HALF, S) if t + 1 < PACK else (0, HALF, S - PH, S)
            for lo, hi in zip(edges, edges[1:]):
                result = ring.tile([P, hi - lo], F32, name="result", bufs=4)
                nc.vector.tensor_tensor(
                    result[:], y[t][:].indirect(pos3_sb[:, lo // 16 : hi // 16]), damp[t][:, lo:hi], ALU.mult
                )
                nc.sync.dma_start(out_rows[:, t, lo:hi], result[:])
